import numpy as np
import ml_dtypes


def mxq(x, axis, fmt="e4m3"):
    dtype, down = {"e4m3": (ml_dtypes.float8_e4m3fn, 7), "e5m2": (ml_dtypes.float8_e5m2, 14)}[fmt]
    v = np.moveaxis(np.asarray(x, np.float32).astype(ml_dtypes.bfloat16).astype(np.float64), axis, -1)
    blocks = v.reshape(v.shape[:-1] + (-1, 32))
    amax = np.abs(blocks).max(-1, keepdims=True)
    byte = np.maximum(np.where(amax > 0, np.frexp(amax)[1] - 1 + 127, 0) - down, 1)
    scale = np.exp2(byte - 127.0)
    codes = (blocks / scale).astype(np.float32).astype(dtype).astype(np.float64)
    return np.moveaxis((codes * scale).reshape(v.shape), -1, axis)


WIDE = False


def mx_kscale(k):
    if not WIDE:
        return np.ones(k)
    levels = np.array([10, -10, 5, -5, 0])
    if k % 512:
        return np.exp2(np.random.permutation(np.resize(levels, k // 32))).repeat(32)
    a = np.empty((k // 512, 16))
    for p in range(k // 512):
        a[p, :8] = np.random.permutation(np.resize(levels, 8))
        for g in range(8):
            far = levels[np.abs(levels - a[p, g]) >= 10]
            a[p, g + 8] = far[np.random.randint(len(far))]
    return np.exp2(a.ravel()).repeat(32)


def f64(x):
    return np.asarray(x).astype(np.float64)


def striped(idx):
    return np.tile(idx.reshape(-1, 16).T, (8, 1)).astype(np.uint16)


def unstriped(offs):
    return offs[:16].T.reshape(-1).astype(np.int64)


def striped8(idx):
    return np.concatenate([x.reshape(-1, 16).T for x in idx]).astype(np.uint16)


def runs(offs, k):
    lists = np.stack([offs[16 * r : 16 * r + 16].T.reshape(-1) for r in range(8)]).astype(np.int64)
    return lists[np.arange(k) % 512 // 64]


def pack_weight(w):
    k, n = w.shape
    w = f64(np.asarray(w, np.float32).astype(ml_dtypes.bfloat16)).reshape(k // 32, 32, n)
    amax = np.abs(w).max(1)
    byte = np.clip(np.where(amax > 0, np.frexp(amax)[1] - 1 + 127 - 7, 1), 1, 254)
    scaled = (w * np.exp2(127.0 - byte)[:, None, :]).reshape(k, n).astype(np.float32)
    words = np.ascontiguousarray(scaled.reshape(k // 512, 128, 4, n).transpose(0, 1, 3, 2)).astype(ml_dtypes.float8_e4m3fn).view(np.uint8)
    return words, np.ascontiguousarray(byte.astype(np.uint8).reshape(k // 512, 16, n))


def unpack_weight(words, scales):
    g, p, n, _ = words.shape
    vals = np.ascontiguousarray(words).view(ml_dtypes.float8_e4m3fn).astype(np.float64) * np.repeat(np.exp2(scales.astype(np.float64) - 127.0), 8, axis=1)[..., None]
    return vals.transpose(0, 1, 3, 2).reshape(g * 512, n)


def sigmoid(v):
    return 1.0 / (1.0 + np.exp(-np.maximum(v, -700.0)))

def planes(y):
    n, m = y.shape
    v = y.astype(np.float32).astype(ml_dtypes.bfloat16).astype(np.float64).reshape(n // 32, 32, m)
    top = np.abs(v).max(1)
    byte = np.clip(np.where(top > 0, np.frexp(top)[1] - 1 + 127 - 7, 1), 1, 254)
    codes = (v * np.exp2(127.0 - byte)[:, None, :]).reshape(n, m).astype(np.float32).astype(ml_dtypes.float8_e4m3fn).view(np.uint8)
    words = codes.reshape(n // 512, 128, 4, m).transpose(0, 1, 3, 2)
    return np.ascontiguousarray(words), np.ascontiguousarray(byte.astype(np.uint8).reshape(n // 512, 16, m))


K, T, S, N, H, W = 512, 2048, 512, 512, 512, 256


def setup_inputs():
    n = np.random.standard_normal
    s = mx_kscale(K)[:, None]
    u = mx_kscale(S)
    packed_xT = pack_weight(n((K, T)) * s)
    packed_w1 = pack_weight(n((S, N)) / np.sqrt(S) / u[:, None])
    perm = np.random.permutation(H)
    return {
        "x_words": packed_xT[0],
        "x_scales": packed_xT[1],
        "wa": (n((K, H)) / np.sqrt(K) / s).astype(np.float32),
        "gt": (np.random.uniform(0.5, 1.5, (S, 1)) * u[:, None]).astype(np.float32),
        "w1_words": packed_w1[0],
        "w1_scales": packed_w1[1],
        "sl": np.random.uniform(1.0, 2.0, (N, 1)).astype(np.float32),
        "th": (0.5 * n((N, 1))).astype(np.float32),
        "offs": striped(np.random.permutation(T)[:S]),
        "n1": striped8(np.stack([np.random.permutation(H) for _ in range(8)])),
        "n2": striped8(np.stack([np.random.permutation(H) for _ in range(8)])),
        "n3": striped8(np.stack([np.random.permutation(H) for _ in range(8)])),
        "n4": striped(perm[:W]),
        "n5": striped(perm[W:]),
    }


def reference(x_words, x_scales, wa, gt, w1_words, w1_scales, sl, th, offs, n1, n2, n3, n4, n5):
    xq = unpack_weight(x_words, x_scales)[:, unstriped(offs)]
    y = xq.T @ mxq(f64(wa), 0, "e4m3")
    z = f64(gt) * ((y[np.arange(S)[:, None], runs(n1, S)]) * sigmoid(y) + (y[np.arange(S)[:, None], runs(n2, S)]) * (sigmoid(y[np.arange(S)[:, None], runs(n3, S)])))
    h = unpack_weight(w1_words, w1_scales).T @ mxq(z, 0, "e4m3")
    pb = h[:, unstriped(n5)]
    sg = sigmoid(f64(sl) * (h[:, unstriped(n4)] - f64(th)))
    rb = pb - sg
    pa = h[:, unstriped(n4)]
    sg2 = sigmoid(f64(sl) * (h[:, unstriped(n5)] - f64(th)))
    ra = pa * sg2
    ds = np.zeros((N, H))
    ds[:, unstriped(n4)] = ra
    out = ds.copy()
    out[:, unstriped(n5)] = rb
    return (out,) + planes(out)

@@ -1,0 +1,222 @@
+from contextlib import ExitStack
+
+import concourse.mybir as mybir
+
+K, T, S, N, H, W = 512, 2048, 512, 512, 512, 256
+FLOPS = 2 * S * K * H + 2 * N * S * H
+
+F32 = mybir.dt.float32
+BF16 = mybir.dt.bfloat16
+I32 = mybir.dt.int32
+U32 = mybir.dt.uint32
+U16 = mybir.dt.uint16
+U8 = mybir.dt.uint8
+FP8X4 = mybir.dt.float8_e4m3fn_x4
+MULT = mybir.AluOpType.mult
+ADD = mybir.AluOpType.add
+SUB = mybir.AluOpType.subtract
+COPY = mybir.ActivationFunctionType.Copy
+SIGMOID = mybir.ActivationFunctionType.Sigmoid
+
+P = 128
+PACK = 4
+
+
+def tile_picked_tokwsumeod_none_po_kernel(
+    tc, x_words, x_scales, wa, gt, w1_words, w1_scales, sl, th, offs, n1, n2, n3, n4, n5, out_0, out_1, out_2
+):
+    nc = tc.nc
+    with ExitStack() as ctx:
+        keep = ctx.enter_context(tc.tile_pool(name="keep", bufs=1))
+        psum = ctx.enter_context(tc.psum_pool(name="psum", bufs=1))
+
+        def sb(shape, dtype, name, tag=None):
+            return keep.tile(shape, dtype, name=name, tag=tag or name, align_bytes=64)
+
+        def load_list(src, name):
+            tile = keep.tile(list(src.shape), U16, name=name)
+            nc.sync.dma_start(tile[:], src)
+            return tile
+
+        def load_rows(queue, src, name):
+            tile = sb([P, PACK], F32, name)
+            queue.dma_start(tile[:], src.rearrange("(p t) o -> p (t o)", t=PACK))
+            return tile
+
+        def load_scale_rows(queue, tile, src):
+            for q in range(4):
+                queue.dma_start(tile[32 * q : 32 * q + 4, :].bitcast(I32), src[0, 4 * q : 4 * q + 4, :].bitcast(I32))
+
+        offs_t = load_list(offs, "offs_t")
+        wa_view = wa.rearrange("(p j) c -> p j c", j=PACK)
+        wa_raw = [sb([P, PACK, W], F32, f"wa_raw{i}") for i in range(2)]
+        xw = sb([P, T], U32, "xw")
+        nc.sync.dma_start(wa_raw[0][:], wa_view[:, :, :W])
+        nc.sync.dma_start(xw[:].bitcast(I32), x_words[0].rearrange("p n t -> p (n t)").bitcast(I32))
+        nc.sync.dma_start(wa_raw[1][:], wa_view[:, :, W:])
+        xs = sb([P, T], U8, "xs")
+        nc.vector.memset(xs[:].bitcast(I32), 0)
+        load_scale_rows(nc.scalar, xs, x_scales)
+        gt_t = load_rows(nc.scalar, gt, "gt_t")
+        w1s_raw = sb([P, N], U8, "w1s_raw")
+        nc.vector.memset(w1s_raw[:].bitcast(I32), 0)
+        n3_t = load_list(n3, "n3_t")
+        n1_t = load_list(n1, "n1_t")
+        n2_t = load_list(n2, "n2_t")
+        w1w_raw = sb([P, N], U32, "w1w_raw")
+        nc.sync.dma_start(w1w_raw[:].bitcast(I32), w1_words[0].rearrange("p n t -> p (n t)").bitcast(I32))
+        load_scale_rows(nc.sync, w1s_raw, w1_scales)
+        n4_t = load_list(n4, "n4_t")
+        n5_t = load_list(n5, "n5_t")
+        sl_t = load_rows(nc.sync, sl, "sl_t")
+        th_t = load_rows(nc.sync, th, "th_t")
+
+        xqs = sb([P, S], U8, "xqs")
+        nc.vector.tensor_copy(xqs[:].rearrange("p (t m) -> p m t", t=PACK), xs[:].indirect(offs_t[:]))
+        xq = sb([P, S], U32, "xq", tag="xs")
+        nc.vector.tensor_copy(xq[:].rearrange("p (t m) -> p m t", t=PACK), xw[:].indirect(offs_t[:]))
+
+        def interleaved(ap):
+            return ap.rearrange("p (c i) t -> p c t i", i=4)
+
+        def planar(ap):
+            return ap.rearrange("p t (c i) -> p c t i", i=4)
+
+        def product(dst, words, scales, t, codes, code_scales):
+            rows = slice(P * t, P * (t + 1))
+            nc.tensor.matmul_mx(
+                dst, lhsT=words[:, rows].bitcast(FP8X4), lhsT_scale=scales[:, rows],
+                rhs=codes[:].bitcast(FP8X4), rhs_scale=code_scales[:], start=True, stop=True,
+            )
+
+        yg = [sb([P, H], F32, f"yg{t}") for t in range(PACK)]
+        sy = [sb([P, H], F32, f"sy{t}") for t in range(PACK)]
+        ybank = {}
+        for i in range(2):
+            wab = sb([P, W, PACK], BF16, f"wab{i}", tag="xw" if i == 1 else None)
+            nc.vector.tensor_copy(interleaved(wab[:]), planar(wa_raw[i][:]))
+            waq = sb([P, W], U32, f"waq{i}")
+            was = sb([P, W], U8, f"was{i}")
+            nc.vector.quantize_mx(waq[:].bitcast(FP8X4), was[:], wab[:].rearrange("p c t -> p (c t)"))
+            for t in range(PACK):
+                ybank[i, t] = psum.tile([P, W], F32, name=f"y{i}_{t}", tag=f"bank{PACK * i + t}")
+                product(ybank[i, t][:], xq, xqs, t, waq, was)
+
+        def half(i):
+            return slice(W * i, W * (i + 1))
+
+        def entries(i):
+            return slice(W // 16 * i, W // 16 * (i + 1))
+
+        def sigmoid_out(i, t):
+            nc.scalar.activation(sy[t][:, half(i)], ybank[i, t][:], SIGMOID)
+
+        def scaled_out(i, t, on_vector=False):
+            if on_vector:
+                nc.vector.tensor_scalar_mul(yg[t][:, half(i)], ybank[i, t][:], gt_t[:, t : t + 1])
+            else:
+                nc.scalar.activation(yg[t][:, half(i)], ybank[i, t][:], COPY, scale=gt_t[:, t : t + 1])
+
+        za = [sb([P, PACK, W], F32, f"za{i}") for i in range(2)]
+        zb = [sb([P, PACK, W], F32, f"zb{i}") for i in range(2)]
+
+        def terms(i, t, split):
+            s3 = sb([P, W], F32, f"s3_{i}_{t}")
+            nc.scalar.activation(s3[:], sy[t][:].indirect(n3_t[:, entries(i)]), COPY)
+            if split:
+                g1 = sb([P, W], F32, f"g1_{i}_{t}")
+                nc.scalar.activation(g1[:], yg[t][:].indirect(n1_t[:, entries(i)]), COPY)
+                nc.vector.tensor_tensor(zb[i][:, t, :], yg[t][:].indirect(n2_t[:, entries(i)]), s3[:], MULT)
+                nc.vector.tensor_tensor(za[i][:, t, :], g1[:], sy[t][:, half(i)], MULT)
+            else:
+                nc.vector.tensor_tensor(za[i][:, t, :], yg[t][:].indirect(n1_t[:, entries(i)]), sy[t][:, half(i)], MULT)
+                nc.vector.tensor_tensor(zb[i][:, t, :], yg[t][:].indirect(n2_t[:, entries(i)]), s3[:], MULT)
+
+        hs = [sb([P, H], F32, f"hs{t}") for t in range(PACK)]
+
+        def add_terms(i, c0, c1):
+            zi = sb([P, c1 - c0, PACK], BF16, f"zi{i}_{c0}")
+            nc.vector.tensor_tensor(interleaved(zi[:]), planar(za[i][:, :, c0:c1]), planar(zb[i][:, :, c0:c1]), ADD)
+            return zi
+
+        hbank = [psum.tile([P, H], F32, name=f"h{t}", tag=f"bank{t}") for t in range(PACK)]
+
+        def second_product(i, c0, c1, zi, first_bank):
+            zq = sb([P, c1 - c0], U32, f"zq{i}_{c0}")
+            zs = sb([P, c1 - c0], U8, f"zs{i}_{c0}")
+            nc.vector.quantize_mx(zq[:].bitcast(FP8X4), zs[:], zi[:].rearrange("p c t -> p (c t)"))
+            cols = slice(W * i + c0, W * i + c1)
+            product(first_bank[:, cols], w1w, w1s, 0, zq, zs)
+            nc.scalar.copy(hs[0][:, cols], first_bank[:, cols])
+            for t in range(1, PACK):
+                product(hbank[t][:, cols], w1w, w1s, t, zq, zs)
+
+        for t in range(2):
+            sigmoid_out(0, t)
+            scaled_out(0, t)
+        sigmoid_out(1, 0)
+        scaled_out(1, 1, True)
+        sigmoid_out(1, 1)
+        scaled_out(1, 0, True)
+        terms(0, 0, False)
+        terms(0, 1, False)
+        for t in range(2, PACK):
+            for i in range(2):
+                sigmoid_out(i, t)
+                scaled_out(i, t)
+            terms(0, t, False)
+
+        w1s = sb([P, N], U8, "w1s")
+        nc.vector.tensor_copy(
+            w1s[:].rearrange("p (t m) -> p t m", t=PACK), w1s_raw[:].rearrange("p (m t) -> p t m", t=PACK)
+        )
+        w1w = sb([P, N], U32, "w1w")
+        bias = sb([P, PACK], F32, "bias")
+        nc.vector.scalar_tensor_tensor(bias[:], sl_t[:], -1.0, th_t[:], MULT, MULT)
+
+        zi0 = add_terms(0, 0, W)
+        terms(1, 0, False)
+        nc.scalar.copy(w1w[:].rearrange("p (t m) -> p t m", t=PACK), w1w_raw[:].rearrange("p (m t) -> p t m", t=PACK))
+        second_product(0, 0, W, zi0, hbank[0])
+        for t in range(1, PACK):
+            terms(1, t, t >= 2)
+        Q = W // 2
+        zi1 = [add_terms(1, Q * u, Q * (u + 1)) for u in range(2)]
+        for u in range(2):
+            spare = psum.tile([P, H], F32, name=f"h0_{u}", tag=f"bank{PACK + u}")
+            second_product(1, Q * u, Q * (u + 1), zi1[u], spare)
+        for t in range(1, PACK):
+            nc.vector.tensor_copy(hs[t][:], hbank[t][:])
+
+        oi = [sb([P, W, PACK], BF16, f"oi{i}") for i in range(2)]
+        out_view = out_0.rearrange("(p t) c -> p t c", t=PACK)
+        for t in range(PACK):
+            col = slice(t, t + 1)
+            pa = sb([P, W], F32, f"pa{t}")
+            pb = sb([P, W], F32, f"pb{t}")
+            sg = sb([P, W], F32, f"sg{t}")
+            sg2 = sb([P, W], F32, f"sg2{t}")
+            ra = sb([P, W], F32, f"ra{t}")
+            rb = sb([P, W], F32, f"rb{t}")
+            res = sb([P, H], F32, f"res{t}")
+            nc.scalar.activation(pa[:], hs[t][:].indirect(n4_t[:]), COPY)
+            nc.scalar.activation(sg2[:], hs[t][:].indirect(n5_t[:]), SIGMOID, bias=bias[:, col], scale=sl_t[:, col])
+            nc.vector.tensor_tensor(ra[:], pa[:], sg2[:], MULT)
+            nc.scalar.activation(pb[:], hs[t][:].indirect(n5_t[:]), COPY)
+            nc.scalar.activation(sg[:], hs[t][:].indirect(n4_t[:]), SIGMOID, bias=bias[:, col], scale=sl_t[:, col])
+            nc.vector.tensor_tensor(rb[:], pb[:], sg[:], SUB)
+            nc.scalar.activation(res[:].indirect(n4_t[:]), ra[:], COPY)
+            nc.scalar.activation(res[:].indirect(n5_t[:]), rb[:], COPY)
+            nc.sync.dma_start(out_view[:, t, :], res[:])
+            for i in range(2):
+                nc.vector.tensor_copy(oi[i][:, :, t], res[:, half(i)])
+
+        oq = [sb([P, W], U32, f"oq{i}") for i in range(2)]
+        os_t = sb([P, H], U8, "os_t")
+        words_out = out_1[0].rearrange("p n t -> p (n t)").bitcast(I32)
+        for i in range(2):
+            nc.vector.quantize_mx(oq[i][:].bitcast(FP8X4), os_t[:, half(i)], oi[i][:].rearrange("p c t -> p (c t)"))
+            nc.scalar.dma_start(words_out[:, half(i)], oq[i][:].bitcast(I32))
+        for q in range(4):
+            queue = nc.sync if q < 3 else nc.scalar
+            queue.dma_start(out_2[0, 4 * q : 4 * q + 4, :].bitcast(I32), os_t[32 * q : 32 * q + 4, :].bitcast(I32))

@@ -47,29 +47,40 @@ def tile_picked_tokwsumeod_none_po_kernel(
             for q in range(4):
                 queue.dma_start(tile[32 * q : 32 * q + 4, :].bitcast(I32), src[0, 4 * q : 4 * q + 4, :].bitcast(I32))
 
-        offs_t = load_list(offs, "offs_t")
-        wa_view = wa.rearrange("(p j) c -> p j c", j=PACK)
-        wa_raw = [sb([P, PACK, W], F32, f"wa_raw{i}") for i in range(2)]
-        xw = sb([P, T], U32, "xw")
-        nc.sync.dma_start(wa_raw[0][:], wa_view[:, :, :W])
-        nc.sync.dma_start(xw[:].bitcast(I32), x_words[0].rearrange("p n t -> p (n t)").bitcast(I32))
-        nc.sync.dma_start(wa_raw[1][:], wa_view[:, :, W:])
         xs = sb([P, T], U8, "xs")
         nc.vector.memset(xs[:].bitcast(I32), 0)
-        load_scale_rows(nc.scalar, xs, x_scales)
-        gt_t = load_rows(nc.scalar, gt, "gt_t")
+        offs_t = load_list(offs, "offs_t")
+        wa_view = wa.rearrange("(p j) c -> p j c", j=PACK)
+        wa_cols = (slice(0, 256), slice(256, H))
+        wa_raw = [sb([P, PACK, c.stop - c.start], F32, f"wa_raw{i}") for i, c in enumerate(wa_cols)]
+        xw = sb([P, T], U32, "xw")
+        nc.sync.dma_start(wa_raw[0][:], wa_view[:, :, wa_cols[0]])
         w1s_raw = sb([P, N], U8, "w1s_raw")
-        nc.vector.memset(w1s_raw[:].bitcast(I32), 0)
+        nc.sync.dma_start(w1s_raw[:].bitcast(I32), w1_scales.bitcast(I32).to_broadcast([P // 16, 16, N // 4]))
+        load_scale_rows(nc.sync, xs, x_scales)
+        nc.sync.dma_start(xw[:].bitcast(I32), x_words[0].rearrange("p n t -> p (n t)").bitcast(I32))
+        nc.sync.dma_start(wa_raw[1][:], wa_view[:, :, wa_cols[1]])
+        gt_t = load_rows(nc.sync, gt, "gt_t")
         n3_t = load_list(n3, "n3_t")
         n1_t = load_list(n1, "n1_t")
         n2_t = load_list(n2, "n2_t")
         w1w_raw = sb([P, N], U32, "w1w_raw")
         nc.sync.dma_start(w1w_raw[:].bitcast(I32), w1_words[0].rearrange("p n t -> p (n t)").bitcast(I32))
-        load_scale_rows(nc.sync, w1s_raw, w1_scales)
         n4_t = load_list(n4, "n4_t")
         n5_t = load_list(n5, "n5_t")
         sl_t = load_rows(nc.sync, sl, "sl_t")
         th_t = load_rows(nc.sync, th, "th_t")
+
+        w1s = sb([P, N], U8, "w1s")
+        nc.vector.tensor_copy(
+            w1s[:].rearrange("p (t m) -> p t m", t=PACK), w1s_raw[:].rearrange("p (m t) -> p t m", t=PACK)
+        )
+        for q in range(1, 4):
+            nc.sync.dma_start(w1s[32 * q : 32 * q + 4, :].bitcast(I32), w1s[4 * q : 4 * q + 4, :].bitcast(I32))
+        bias = sb([P, PACK], F32, "bias")
+        sl_th = sb([P, PACK], F32, "sl_th")
+        nc.gpsimd.tensor_tensor(sl_th[:], sl_t[:], th_t[:], MULT)
+        nc.gpsimd.tensor_scalar(bias[:], sl_th[:], -1.0, 0.0, MULT, ADD)
 
         xqs = sb([P, S], U8, "xqs")
         nc.vector.tensor_copy(xqs[:].rearrange("p (t m) -> p m t", t=PACK), xs[:].indirect(offs_t[:]))
@@ -86,130 +97,158 @@ def tile_picked_tokwsumeod_none_po_kernel(
             rows = slice(P * t, P * (t + 1))
             nc.tensor.matmul_mx(
                 dst, lhsT=words[:, rows].bitcast(FP8X4), lhsT_scale=scales[:, rows],
-                rhs=codes[:].bitcast(FP8X4), rhs_scale=code_scales[:], start=True, stop=True,
+                rhs=codes.bitcast(FP8X4), rhs_scale=code_scales, start=True, stop=True,
             )
 
-        yg = [sb([P, H], F32, f"yg{t}") for t in range(PACK)]
-        sy = [sb([P, H], F32, f"sy{t}") for t in range(PACK)]
         ybank = {}
-        for i in range(2):
-            wab = sb([P, W, PACK], BF16, f"wab{i}", tag="xw" if i == 1 else None)
+        wa_mx = []
+        for i, c in enumerate(wa_cols):
+            w = c.stop - c.start
+            wab = sb([P, w, PACK], BF16, f"wab{i}", tag="xw" if i == 1 else None)
             nc.vector.tensor_copy(interleaved(wab[:]), planar(wa_raw[i][:]))
-            waq = sb([P, W], U32, f"waq{i}")
-            was = sb([P, W], U8, f"was{i}")
+            waq = sb([P, w], U32, f"waq{i}")
+            was = sb([P, w], U8, f"was{i}")
             nc.vector.quantize_mx(waq[:].bitcast(FP8X4), was[:], wab[:].rearrange("p c t -> p (c t)"))
-            for t in range(PACK):
-                ybank[i, t] = psum.tile([P, W], F32, name=f"y{i}_{t}", tag=f"bank{PACK * i + t}")
-                product(ybank[i, t][:], xq, xqs, t, waq, was)
+            wa_mx.append((waq, was))
 
-        def half(i):
-            return slice(W * i, W * (i + 1))
+        yg = [sb([P, H], F32, f"yg{t}", tag="xw" if t == 1 else None) for t in range(PACK)]
+        sy = [sb([P, H], F32, f"sy{t}") for t in range(PACK)]
 
-        def entries(i):
-            return slice(W // 16 * i, W // 16 * (i + 1))
+        def first_product(i, t):
+            slot = 2 * i + t
+            waq, was = wa_mx[i]
+            w = waq.shape[1]
+            ybank[i, t] = psum.tile([P, w], F32, name=f"y{i}_{t}", tag=f"bank{slot}")
+            for c0 in range(0, w, W):
+                c = slice(c0, min(c0 + W, w))
+                product(ybank[i, t][:, c], xq, xqs, t, waq[:, c], was[:, c])
 
         def sigmoid_out(i, t):
-            nc.scalar.activation(sy[t][:, half(i)], ybank[i, t][:], SIGMOID)
+            nc.scalar.activation(sy[t][:, wa_cols[i]], ybank[i, t][:], SIGMOID)
 
         def scaled_out(i, t, on_vector=False):
             if on_vector:
-                nc.vector.tensor_scalar_mul(yg[t][:, half(i)], ybank[i, t][:], gt_t[:, t : t + 1])
+                nc.vector.tensor_scalar_mul(yg[t][:, wa_cols[i]], ybank[i, t][:], gt_t[:, t : t + 1])
             else:
-                nc.scalar.activation(yg[t][:, half(i)], ybank[i, t][:], COPY, scale=gt_t[:, t : t + 1])
+                nc.scalar.activation(yg[t][:, wa_cols[i]], ybank[i, t][:], COPY, scale=gt_t[:, t : t + 1])
 
-        za = [sb([P, PACK, W], F32, f"za{i}") for i in range(2)]
-        zb = [sb([P, PACK, W], F32, f"zb{i}") for i in range(2)]
+        z_cols = (slice(0, W), slice(W, H))
+        za = [sb([P, PACK, c.stop - c.start], F32, f"za{i}") for i, c in enumerate(z_cols)]
+        zb = [sb([P, PACK, c.stop - c.start], F32, f"zb{i}") for i, c in enumerate(z_cols)]
 
         def terms(i, t, split):
-            s3 = sb([P, W], F32, f"s3_{i}_{t}")
-            nc.scalar.activation(s3[:], sy[t][:].indirect(n3_t[:, entries(i)]), COPY)
+            c = z_cols[i]
+            w = c.stop - c.start
+            entries = slice(c.start // 16, c.stop // 16)
+            s3 = sb([P, w], F32, f"s3_{i}_{t}")
+            nc.scalar.activation(s3[:], sy[t][:].indirect(n3_t[:, entries]), COPY)
             if split:
-                g1 = sb([P, W], F32, f"g1_{i}_{t}")
-                nc.scalar.activation(g1[:], yg[t][:].indirect(n1_t[:, entries(i)]), COPY)
-                nc.vector.tensor_tensor(zb[i][:, t, :], yg[t][:].indirect(n2_t[:, entries(i)]), s3[:], MULT)
-                nc.vector.tensor_tensor(za[i][:, t, :], g1[:], sy[t][:, half(i)], MULT)
+                g1 = sb([P, w], F32, f"g1_{i}_{t}")
+                nc.scalar.activation(g1[:], yg[t][:].indirect(n1_t[:, entries]), COPY)
+                nc.vector.tensor_tensor(zb[i][:, t, :], yg[t][:].indirect(n2_t[:, entries]), s3[:], MULT)
+                nc.vector.tensor_tensor(za[i][:, t, :], g1[:], sy[t][:, c], MULT)
             else:
-                nc.vector.tensor_tensor(za[i][:, t, :], yg[t][:].indirect(n1_t[:, entries(i)]), sy[t][:, half(i)], MULT)
-                nc.vector.tensor_tensor(zb[i][:, t, :], yg[t][:].indirect(n2_t[:, entries(i)]), s3[:], MULT)
+                nc.vector.tensor_tensor(za[i][:, t, :], yg[t][:].indirect(n1_t[:, entries]), sy[t][:, c], MULT)
+                nc.vector.tensor_tensor(zb[i][:, t, :], yg[t][:].indirect(n2_t[:, entries]), s3[:], MULT)
 
         hs = [sb([P, H], F32, f"hs{t}") for t in range(PACK)]
+        hbank = [psum.tile([P, H], F32, name=f"h{t}", tag=f"bank{PACK + t}") for t in range(PACK)]
 
         def add_terms(i, c0, c1):
             zi = sb([P, c1 - c0, PACK], BF16, f"zi{i}_{c0}")
             nc.vector.tensor_tensor(interleaved(zi[:]), planar(za[i][:, :, c0:c1]), planar(zb[i][:, :, c0:c1]), ADD)
             return zi
 
-        hbank = [psum.tile([P, H], F32, name=f"h{t}", tag=f"bank{t}") for t in range(PACK)]
+        zq = [sb([P, W], U32, f"zq{i}") for i in range(2)]
+        zs = [sb([P, W], U8, f"zs{i}") for i in range(2)]
 
-        def second_product(i, c0, c1, zi, first_bank):
-            zq = sb([P, c1 - c0], U32, f"zq{i}_{c0}")
-            zs = sb([P, c1 - c0], U8, f"zs{i}_{c0}")
-            nc.vector.quantize_mx(zq[:].bitcast(FP8X4), zs[:], zi[:].rearrange("p c t -> p (c t)"))
-            cols = slice(W * i + c0, W * i + c1)
-            product(first_bank[:, cols], w1w, w1s, 0, zq, zs)
-            nc.scalar.copy(hs[0][:, cols], first_bank[:, cols])
+        def first_rows(i, c0, c1, zi, bank):
+            nc.vector.quantize_mx(zq[i][:, c0:c1].bitcast(FP8X4), zs[i][:, c0:c1], zi[:].rearrange("p c t -> p (c t)"))
+            cols = slice(z_cols[i].start + c0, z_cols[i].start + c1)
+            product(bank[:, cols], w1w, w1s, 0, zq[i][:, c0:c1], zs[i][:, c0:c1])
+            nc.scalar.copy(hs[0][:, cols], bank[:, cols])
+
+        def other_rows(i):
             for t in range(1, PACK):
-                product(hbank[t][:, cols], w1w, w1s, t, zq, zs)
+                product(hbank[t][:, z_cols[i]], w1w, w1s, t, zq[i][:], zs[i][:])
 
-        for t in range(2):
-            sigmoid_out(0, t)
-            scaled_out(0, t)
+        def spare_bank(u):
+            return psum.tile([P, H], F32, name=f"h0_{u}", tag=f"bank{u}")
+
+        first_product(0, 0)
+        first_product(0, 1)
+        first_product(1, 0)
+        first_product(1, 1)
+        sigmoid_out(0, 0)
+        sigmoid_out(0, 1)
+        scaled_out(0, 0)
+        scaled_out(0, 1, True)
         sigmoid_out(1, 0)
         scaled_out(1, 1, True)
-        sigmoid_out(1, 1)
         scaled_out(1, 0, True)
         terms(0, 0, False)
+        sigmoid_out(1, 1)
         terms(0, 1, False)
         for t in range(2, PACK):
+            whole = psum.tile([P, H], F32, name=f"y{t}", tag=f"bank{t - 2}")
             for i in range(2):
-                sigmoid_out(i, t)
-                scaled_out(i, t)
+                product(whole[:, wa_cols[i]], xq, xqs, t, wa_mx[i][0][:], wa_mx[i][1][:])
+            nc.scalar.activation(sy[t][:], whole[:], SIGMOID)
+            nc.scalar.activation(yg[t][:], whole[:], COPY, scale=gt_t[:, t : t + 1])
             terms(0, t, False)
 
-        w1s = sb([P, N], U8, "w1s")
-        nc.vector.tensor_copy(
-            w1s[:].rearrange("p (t m) -> p t m", t=PACK), w1s_raw[:].rearrange("p (m t) -> p t m", t=PACK)
-        )
-        w1w = sb([P, N], U32, "w1w")
-        bias = sb([P, PACK], F32, "bias")
-        nc.vector.scalar_tensor_tensor(bias[:], sl_t[:], -1.0, th_t[:], MULT, MULT)
-
         zi0 = add_terms(0, 0, W)
-        terms(1, 0, False)
+        for t in range(PACK):
+            terms(1, t, t >= 1)
+        w1w = sb([P, N], U32, "w1w", tag="s3_1_0")
         nc.scalar.copy(w1w[:].rearrange("p (t m) -> p t m", t=PACK), w1w_raw[:].rearrange("p (m t) -> p t m", t=PACK))
-        second_product(0, 0, W, zi0, hbank[0])
-        for t in range(1, PACK):
-            terms(1, t, t >= 2)
+        first_rows(0, 0, W, zi0, hbank[0])
+        other_rows(0)
         Q = W // 2
         zi1 = [add_terms(1, Q * u, Q * (u + 1)) for u in range(2)]
         for u in range(2):
-            spare = psum.tile([P, H], F32, name=f"h0_{u}", tag=f"bank{PACK + u}")
-            second_product(1, Q * u, Q * (u + 1), zi1[u], spare)
+            first_rows(1, Q * u, Q * (u + 1), zi1[u], spare_bank(u))
+        other_rows(1)
         for t in range(1, PACK):
             nc.vector.tensor_copy(hs[t][:], hbank[t][:])
 
+        def half(i):
+            return slice(W * i, W * (i + 1))
+
         oi = [sb([P, W, PACK], BF16, f"oi{i}") for i in range(2)]
         out_view = out_0.rearrange("(p t) c -> p t c", t=PACK)
-        for t in range(PACK):
+        ra = [sb([P, W], F32, f"ra{t}") for t in range(PACK)]
+        rb = [sb([P, W], F32, f"rb{t}") for t in range(PACK)]
+        res = [sb([P, H], F32, f"res{t}") for t in range(PACK)]
+
+        def fetch(t):
             col = slice(t, t + 1)
             pa = sb([P, W], F32, f"pa{t}")
             pb = sb([P, W], F32, f"pb{t}")
             sg = sb([P, W], F32, f"sg{t}")
             sg2 = sb([P, W], F32, f"sg2{t}")
-            ra = sb([P, W], F32, f"ra{t}")
-            rb = sb([P, W], F32, f"rb{t}")
-            res = sb([P, H], F32, f"res{t}")
             nc.scalar.activation(pa[:], hs[t][:].indirect(n4_t[:]), COPY)
             nc.scalar.activation(sg2[:], hs[t][:].indirect(n5_t[:]), SIGMOID, bias=bias[:, col], scale=sl_t[:, col])
-            nc.vector.tensor_tensor(ra[:], pa[:], sg2[:], MULT)
+            nc.vector.tensor_tensor(ra[t][:], pa[:], sg2[:], MULT)
             nc.scalar.activation(pb[:], hs[t][:].indirect(n5_t[:]), COPY)
             nc.scalar.activation(sg[:], hs[t][:].indirect(n4_t[:]), SIGMOID, bias=bias[:, col], scale=sl_t[:, col])
-            nc.vector.tensor_tensor(rb[:], pb[:], sg[:], SUB)
-            nc.scalar.activation(res[:].indirect(n4_t[:]), ra[:], COPY)
-            nc.scalar.activation(res[:].indirect(n5_t[:]), rb[:], COPY)
-            nc.sync.dma_start(out_view[:, t, :], res[:])
+            nc.vector.tensor_tensor(rb[t][:], pb[:], sg[:], SUB)
+
+        def put_a(t):
+            nc.scalar.activation(res[t][:].indirect(n4_t[:]), ra[t][:], COPY)
+
+        def put_b(t):
+            nc.scalar.activation(res[t][:].indirect(n5_t[:]), rb[t][:], COPY)
+            nc.sync.dma_start(out_view[:, t, :], res[t][:])
             for i in range(2):
-                nc.vector.tensor_copy(oi[i][:, :, t], res[:, half(i)])
+                nc.vector.tensor_copy(oi[i][:, :, t], res[t][:, half(i)])
+
+        for t in range(PACK):
+            fetch(t)
+            put_a(t)
+            if t > 0:
+                put_b(t - 1)
+        put_b(PACK - 1)
 
         oq = [sb([P, W], U32, f"oq{i}") for i in range(2)]
         os_t = sb([P, H], U8, "os_t")

from contextlib import ExitStack

import concourse.mybir as mybir

K, T, S, N, H, W = 512, 2048, 512, 512, 512, 256
FLOPS = 2 * S * K * H + 2 * N * S * H

F32 = mybir.dt.float32
BF16 = mybir.dt.bfloat16
I32 = mybir.dt.int32
U32 = mybir.dt.uint32
U16 = mybir.dt.uint16
U8 = mybir.dt.uint8
FP8X4 = mybir.dt.float8_e4m3fn_x4
MULT = mybir.AluOpType.mult
ADD = mybir.AluOpType.add
SUB = mybir.AluOpType.subtract
COPY = mybir.ActivationFunctionType.Copy
SIGMOID = mybir.ActivationFunctionType.Sigmoid

P = 128
PACK = 4


def tile_picked_tokwsumeod_none_po_kernel(
    tc, x_words, x_scales, wa, gt, w1_words, w1_scales, sl, th, offs, n1, n2, n3, n4, n5, out_0, out_1, out_2
):
    nc = tc.nc
    with ExitStack() as ctx:
        keep = ctx.enter_context(tc.tile_pool(name="keep", bufs=1))
        psum = ctx.enter_context(tc.psum_pool(name="psum", bufs=1))

        def sb(shape, dtype, name, tag=None):
            return keep.tile(shape, dtype, name=name, tag=tag or name, align_bytes=64)

        def load_list(src, name):
            tile = keep.tile(list(src.shape), U16, name=name)
            nc.sync.dma_start(tile[:], src)
            return tile

        def load_rows(queue, src, name):
            tile = sb([P, PACK], F32, name)
            queue.dma_start(tile[:], src.rearrange("(p t) o -> p (t o)", t=PACK))
            return tile

        def load_scale_rows(queue, tile, src):
            for q in range(4):
                queue.dma_start(tile[32 * q : 32 * q + 4, :].bitcast(I32), src[0, 4 * q : 4 * q + 4, :].bitcast(I32))

        xs = sb([P, T], U8, "xs")
        nc.vector.memset(xs[:].bitcast(I32), 0)
        offs_t = load_list(offs, "offs_t")
        wa_view = wa.rearrange("(p j) c -> p j c", j=PACK)
        wa_cols = (slice(0, 256), slice(256, H))
        wa_raw = [sb([P, PACK, c.stop - c.start], F32, f"wa_raw{i}") for i, c in enumerate(wa_cols)]
        xw = sb([P, T], U32, "xw")
        nc.sync.dma_start(wa_raw[0][:], wa_view[:, :, wa_cols[0]])
        w1s_raw = sb([P, N], U8, "w1s_raw")
        nc.sync.dma_start(w1s_raw[:].bitcast(I32), w1_scales.bitcast(I32).to_broadcast([P // 16, 16, N // 4]))
        load_scale_rows(nc.sync, xs, x_scales)
        nc.sync.dma_start(xw[:].bitcast(I32), x_words[0].rearrange("p n t -> p (n t)").bitcast(I32))
        nc.sync.dma_start(wa_raw[1][:], wa_view[:, :, wa_cols[1]])
        gt_t = load_rows(nc.sync, gt, "gt_t")
        n3_t = load_list(n3, "n3_t")
        n1_t = load_list(n1, "n1_t")
        n2_t = load_list(n2, "n2_t")
        w1w_raw = sb([P, N], U32, "w1w_raw")
        nc.sync.dma_start(w1w_raw[:].bitcast(I32), w1_words[0].rearrange("p n t -> p (n t)").bitcast(I32))
        n4_t = load_list(n4, "n4_t")
        n5_t = load_list(n5, "n5_t")
        sl_t = load_rows(nc.sync, sl, "sl_t")
        th_t = load_rows(nc.sync, th, "th_t")

        w1s = sb([P, N], U8, "w1s")
        nc.vector.tensor_copy(
            w1s[:].rearrange("p (t m) -> p t m", t=PACK), w1s_raw[:].rearrange("p (m t) -> p t m", t=PACK)
        )
        for q in range(1, 4):
            nc.sync.dma_start(w1s[32 * q : 32 * q + 4, :].bitcast(I32), w1s[4 * q : 4 * q + 4, :].bitcast(I32))
        bias = sb([P, PACK], F32, "bias")
        sl_th = sb([P, PACK], F32, "sl_th")
        nc.gpsimd.tensor_tensor(sl_th[:], sl_t[:], th_t[:], MULT)
        nc.gpsimd.tensor_scalar(bias[:], sl_th[:], -1.0, 0.0, MULT, ADD)

        xqs = sb([P, S], U8, "xqs")
        nc.vector.tensor_copy(xqs[:].rearrange("p (t m) -> p m t", t=PACK), xs[:].indirect(offs_t[:]))
        xq = sb([P, S], U32, "xq", tag="xs")
        nc.vector.tensor_copy(xq[:].rearrange("p (t m) -> p m t", t=PACK), xw[:].indirect(offs_t[:]))

        def interleaved(ap):
            return ap.rearrange("p (c i) t -> p c t i", i=4)

        def planar(ap):
            return ap.rearrange("p t (c i) -> p c t i", i=4)

        def product(dst, words, scales, t, codes, code_scales):
            rows = slice(P * t, P * (t + 1))
            nc.tensor.matmul_mx(
                dst, lhsT=words[:, rows].bitcast(FP8X4), lhsT_scale=scales[:, rows],
                rhs=codes.bitcast(FP8X4), rhs_scale=code_scales, start=True, stop=True,
            )

        ybank = {}
        wa_mx = []
        for i, c in enumerate(wa_cols):
            w = c.stop - c.start
            wab = sb([P, w, PACK], BF16, f"wab{i}", tag="xw" if i == 1 else None)
            nc.vector.tensor_copy(interleaved(wab[:]), planar(wa_raw[i][:]))
            waq = sb([P, w], U32, f"waq{i}")
            was = sb([P, w], U8, f"was{i}")
            nc.vector.quantize_mx(waq[:].bitcast(FP8X4), was[:], wab[:].rearrange("p c t -> p (c t)"))
            wa_mx.append((waq, was))

        yg = [sb([P, H], F32, f"yg{t}", tag="xw" if t == 1 else None) for t in range(PACK)]
        sy = [sb([P, H], F32, f"sy{t}") for t in range(PACK)]

        def first_product(i, t):
            slot = 2 * i + t
            waq, was = wa_mx[i]
            w = waq.shape[1]
            ybank[i, t] = psum.tile([P, w], F32, name=f"y{i}_{t}", tag=f"bank{slot}")
            for c0 in range(0, w, W):
                c = slice(c0, min(c0 + W, w))
                product(ybank[i, t][:, c], xq, xqs, t, waq[:, c], was[:, c])

        def sigmoid_out(i, t):
            nc.scalar.activation(sy[t][:, wa_cols[i]], ybank[i, t][:], SIGMOID)

        def scaled_out(i, t, on_vector=False):
            if on_vector:
                nc.vector.tensor_scalar_mul(yg[t][:, wa_cols[i]], ybank[i, t][:], gt_t[:, t : t + 1])
            else:
                nc.scalar.activation(yg[t][:, wa_cols[i]], ybank[i, t][:], COPY, scale=gt_t[:, t : t + 1])

        z_cols = (slice(0, W), slice(W, H))
        za = [sb([P, PACK, c.stop - c.start], F32, f"za{i}") for i, c in enumerate(z_cols)]
        zb = [sb([P, PACK, c.stop - c.start], F32, f"zb{i}") for i, c in enumerate(z_cols)]

        def terms(i, t, split):
            c = z_cols[i]
            w = c.stop - c.start
            entries = slice(c.start // 16, c.stop // 16)
            s3 = sb([P, w], F32, f"s3_{i}_{t}")
            nc.scalar.activation(s3[:], sy[t][:].indirect(n3_t[:, entries]), COPY)
            if split:
                g1 = sb([P, w], F32, f"g1_{i}_{t}")
                nc.scalar.activation(g1[:], yg[t][:].indirect(n1_t[:, entries]), COPY)
                nc.vector.tensor_tensor(zb[i][:, t, :], yg[t][:].indirect(n2_t[:, entries]), s3[:], MULT)
                nc.vector.tensor_tensor(za[i][:, t, :], g1[:], sy[t][:, c], MULT)
            else:
                nc.vector.tensor_tensor(za[i][:, t, :], yg[t][:].indirect(n1_t[:, entries]), sy[t][:, c], MULT)
                nc.vector.tensor_tensor(zb[i][:, t, :], yg[t][:].indirect(n2_t[:, entries]), s3[:], MULT)

        hs = [sb([P, H], F32, f"hs{t}") for t in range(PACK)]
        hbank = [psum.tile([P, H], F32, name=f"h{t}", tag=f"bank{PACK + t}") for t in range(PACK)]

        def add_terms(i, c0, c1):
            zi = sb([P, c1 - c0, PACK], BF16, f"zi{i}_{c0}")
            nc.vector.tensor_tensor(interleaved(zi[:]), planar(za[i][:, :, c0:c1]), planar(zb[i][:, :, c0:c1]), ADD)
            return zi

        zq = [sb([P, W], U32, f"zq{i}") for i in range(2)]
        zs = [sb([P, W], U8, f"zs{i}") for i in range(2)]

        def first_rows(i, c0, c1, zi, bank):
            nc.vector.quantize_mx(zq[i][:, c0:c1].bitcast(FP8X4), zs[i][:, c0:c1], zi[:].rearrange("p c t -> p (c t)"))
            cols = slice(z_cols[i].start + c0, z_cols[i].start + c1)
            product(bank[:, cols], w1w, w1s, 0, zq[i][:, c0:c1], zs[i][:, c0:c1])
            nc.scalar.copy(hs[0][:, cols], bank[:, cols])

        def other_rows(i):
            for t in range(1, PACK):
                product(hbank[t][:, z_cols[i]], w1w, w1s, t, zq[i][:], zs[i][:])

        def spare_bank(u):
            return psum.tile([P, H], F32, name=f"h0_{u}", tag=f"bank{u}")

        first_product(0, 0)
        first_product(0, 1)
        first_product(1, 0)
        first_product(1, 1)
        sigmoid_out(0, 0)
        sigmoid_out(0, 1)
        scaled_out(0, 0)
        scaled_out(0, 1, True)
        sigmoid_out(1, 0)
        scaled_out(1, 1, True)
        scaled_out(1, 0, True)
        terms(0, 0, False)
        sigmoid_out(1, 1)
        terms(0, 1, False)
        for t in range(2, PACK):
            whole = psum.tile([P, H], F32, name=f"y{t}", tag=f"bank{t - 2}")
            for i in range(2):
                product(whole[:, wa_cols[i]], xq, xqs, t, wa_mx[i][0][:], wa_mx[i][1][:])
            nc.scalar.activation(sy[t][:], whole[:], SIGMOID)
            nc.scalar.activation(yg[t][:], whole[:], COPY, scale=gt_t[:, t : t + 1])
            terms(0, t, False)

        zi0 = add_terms(0, 0, W)
        for t in range(PACK):
            terms(1, t, t >= 1)
        w1w = sb([P, N], U32, "w1w", tag="s3_1_0")
        nc.scalar.copy(w1w[:].rearrange("p (t m) -> p t m", t=PACK), w1w_raw[:].rearrange("p (m t) -> p t m", t=PACK))
        first_rows(0, 0, W, zi0, hbank[0])
        other_rows(0)
        Q = W // 2
        zi1 = [add_terms(1, Q * u, Q * (u + 1)) for u in range(2)]
        for u in range(2):
            first_rows(1, Q * u, Q * (u + 1), zi1[u], spare_bank(u))
        other_rows(1)
        for t in range(1, PACK):
            nc.vector.tensor_copy(hs[t][:], hbank[t][:])

        def half(i):
            return slice(W * i, W * (i + 1))

        oi = [sb([P, W, PACK], BF16, f"oi{i}") for i in range(2)]
        out_view = out_0.rearrange("(p t) c -> p t c", t=PACK)
        ra = [sb([P, W], F32, f"ra{t}") for t in range(PACK)]
        rb = [sb([P, W], F32, f"rb{t}") for t in range(PACK)]
        res = [sb([P, H], F32, f"res{t}") for t in range(PACK)]

        def fetch(t):
            col = slice(t, t + 1)
            pa = sb([P, W], F32, f"pa{t}")
            pb = sb([P, W], F32, f"pb{t}")
            sg = sb([P, W], F32, f"sg{t}")
            sg2 = sb([P, W], F32, f"sg2{t}")
            nc.scalar.activation(pa[:], hs[t][:].indirect(n4_t[:]), COPY)
            nc.scalar.activation(sg2[:], hs[t][:].indirect(n5_t[:]), SIGMOID, bias=bias[:, col], scale=sl_t[:, col])
            nc.vector.tensor_tensor(ra[t][:], pa[:], sg2[:], MULT)
            nc.scalar.activation(pb[:], hs[t][:].indirect(n5_t[:]), COPY)
            nc.scalar.activation(sg[:], hs[t][:].indirect(n4_t[:]), SIGMOID, bias=bias[:, col], scale=sl_t[:, col])
            nc.vector.tensor_tensor(rb[t][:], pb[:], sg[:], SUB)

        def put_a(t):
            nc.scalar.activation(res[t][:].indirect(n4_t[:]), ra[t][:], COPY)

        def put_b(t):
            nc.scalar.activation(res[t][:].indirect(n5_t[:]), rb[t][:], COPY)
            nc.sync.dma_start(out_view[:, t, :], res[t][:])
            for i in range(2):
                nc.vector.tensor_copy(oi[i][:, :, t], res[t][:, half(i)])

        for t in range(PACK):
            fetch(t)
            put_a(t)
            if t > 0:
                put_b(t - 1)
        put_b(PACK - 1)

        oq = [sb([P, W], U32, f"oq{i}") for i in range(2)]
        os_t = sb([P, H], U8, "os_t")
        words_out = out_1[0].rearrange("p n t -> p (n t)").bitcast(I32)
        for i in range(2):
            nc.vector.quantize_mx(oq[i][:].bitcast(FP8X4), os_t[:, half(i)], oi[i][:].rearrange("p c t -> p (c t)"))
            nc.scalar.dma_start(words_out[:, half(i)], oq[i][:].bitcast(I32))
        for q in range(4):
            queue = nc.sync if q < 3 else nc.scalar
            queue.dma_start(out_2[0, 4 * q : 4 * q + 4, :].bitcast(I32), os_t[32 * q : 32 * q + 4, :].bitcast(I32))
